import numpy as np
import ml_dtypes


def mxq(x, axis, fmt="e4m3"):
    dtype, down = {"e4m3": (ml_dtypes.float8_e4m3fn, 7), "e5m2": (ml_dtypes.float8_e5m2, 14)}[fmt]
    v = np.moveaxis(np.asarray(x, np.float32).astype(ml_dtypes.bfloat16).astype(np.float64), axis, -1)
    blocks = v.reshape(v.shape[:-1] + (-1, 32))
    amax = np.abs(blocks).max(-1, keepdims=True)
    byte = np.maximum(np.where(amax > 0, np.frexp(amax)[1] - 1 + 127, 0) - down, 1)
    scale = np.exp2(byte - 127.0)
    codes = (blocks / scale).astype(np.float32).astype(dtype).astype(np.float64)
    return np.moveaxis((codes * scale).reshape(v.shape), -1, axis)


WIDE = False


def mx_kscale(k):
    if not WIDE:
        return np.ones(k)
    levels = np.array([10, -10, 5, -5, 0])
    if k % 512:
        return np.exp2(np.random.permutation(np.resize(levels, k // 32))).repeat(32)
    a = np.empty((k // 512, 16))
    for p in range(k // 512):
        a[p, :8] = np.random.permutation(np.resize(levels, 8))
        for g in range(8):
            far = levels[np.abs(levels - a[p, g]) >= 10]
            a[p, g + 8] = far[np.random.randint(len(far))]
    return np.exp2(a.ravel()).repeat(32)


def f64(x):
    return np.asarray(x).astype(np.float64)


def striped(idx):
    return np.tile(idx.reshape(-1, 16).T, (8, 1)).astype(np.uint16)


def unstriped(offs):
    return offs[:16].T.reshape(-1).astype(np.int64)


def pack_weight(w):
    k, n = w.shape
    w = f64(np.asarray(w, np.float32).astype(ml_dtypes.bfloat16)).reshape(k // 32, 32, n)
    amax = np.abs(w).max(1)
    byte = np.clip(np.where(amax > 0, np.frexp(amax)[1] - 1 + 127 - 7, 1), 1, 254)
    scaled = (w * np.exp2(127.0 - byte)[:, None, :]).reshape(k, n).astype(np.float32)
    words = np.ascontiguousarray(scaled.reshape(k // 512, 128, 4, n).transpose(0, 1, 3, 2)).astype(ml_dtypes.float8_e4m3fn).view(np.uint8)
    return words, np.ascontiguousarray(byte.astype(np.uint8).reshape(k // 512, 16, n))


def unpack_weight(words, scales):
    g, p, n, _ = words.shape
    vals = np.ascontiguousarray(words).view(ml_dtypes.float8_e4m3fn).astype(np.float64) * np.repeat(np.exp2(scales.astype(np.float64) - 127.0), 8, axis=1)[..., None]
    return vals.transpose(0, 1, 3, 2).reshape(g * 512, n)


def relu(v):
    return np.maximum(v, 0.0)


K, T, S, N, D = 1024, 2048, 512, 128, 3
P = 2 ** 7


def setup_inputs():
    n = np.random.standard_normal
    s = mx_kscale(K)[:, None]
    packed_xT = pack_weight(n((K, T)) * s)
    return {
        "x_words": packed_xT[0],
        "x_scales": packed_xT[1],
        "w1": (n((K, N)) / np.sqrt(K) / s).astype(np.float32),
        "cond": (np.tile(np.random.uniform(0.05, 0.25, (D, 1, S)), (1, P, 1))).astype(np.float32),
        "offs": striped(np.random.permutation(T)[:S]),
        "pos1": striped(np.random.permutation(S)[:S]),
        "pos2": striped(np.random.permutation(S)[:S]),
        "pos3": striped(np.random.permutation(S)[:S]),
    }


def reference(x_words, x_scales, w1, cond, offs, pos1, pos2, pos3):
    xq = unpack_weight(x_words, x_scales)[:, unstriped(offs)]
    y = mxq(f64(w1), 0, "e4m3").T @ xq
    tm0 = relu(y - 0.6) - relu(-1.0 * y)
    ent = y + (tm0[:, unstriped(pos1)] - tm0) * f64(cond)[0, :1] + (tm0[:, unstriped(pos2)] - tm0) * f64(cond)[1, :1] + (tm0[:, unstriped(pos3)] - tm0) * f64(cond)[2, :1]
    tm1 = relu(ent - 0.6) - relu(-1.0 * ent)
    return ent + (tm1[:, unstriped(pos1)] - tm1) * f64(cond)[0, :1] + (tm1[:, unstriped(pos2)] - tm1) * f64(cond)[1, :1] + (tm1[:, unstriped(pos3)] - tm1) * f64(cond)[2, :1]

@@ -1,0 +1,164 @@
+from contextlib import ExitStack
+
+import concourse.mybir as mybir
+from concourse.masks import make_identity
+
+K, T, S, N, D = 1024, 2048, 512, 128, 3
+FLOPS = 2 * K * S * N
+
+F32 = mybir.dt.float32
+BF16 = mybir.dt.bfloat16
+I32 = mybir.dt.int32
+U32 = mybir.dt.uint32
+U16 = mybir.dt.uint16
+U8 = mybir.dt.uint8
+FP8X4 = mybir.dt.float8_e4m3fn_x4
+ALU = mybir.AluOpType
+ACT = mybir.ActivationFunctionType
+
+P = 128
+PACK = 4
+PASSES = K // (P * PACK)
+HALF = S // 2
+BLOCKS = S // P
+LATENT = 0.6
+
+
+def tile_picked_ystefn_two_p_kernel(tc, x_words, x_scales, w1, cond, offs, pos1, pos2, pos3, out):
+    nc = tc.nc
+    with ExitStack() as ctx:
+        keep = ctx.enter_context(tc.tile_pool(name="keep", bufs=1))
+        psum = ctx.enter_context(tc.psum_pool(name="psum", bufs=1))
+
+        def cols(h):
+            return slice(h * HALF, (h + 1) * HALF)
+
+        def entries(h):
+            return slice(h * HALF // 16, (h + 1) * HALF // 16)
+
+        def block(b):
+            return slice(b * P, (b + 1) * P)
+
+        scale_table = keep.tile([P, T], U8, name="scale_table", align_bytes=64)
+        nc.vector.memset(scale_table[:].bitcast(I32), 0)
+        cond_rows = keep.tile([P, D, P], F32, name="cond_rows")
+        nc.vector.memset(cond_rows[:], 0.0)
+        ident = keep.tile([P, P], F32, name="ident")
+        make_identity(nc, ident[:])
+
+        w_raw = keep.tile([P, PASSES, PACK, N], F32, name="w_raw")
+        nc.sync.dma_start(w_raw[:], w1.rearrange("(g p t) n -> p g t n", g=PASSES, t=PACK))
+        for q in range(4):
+            nc.sync.dma_start(
+                scale_table[32 * q : 32 * q + 4 * PASSES, :].bitcast(I32),
+                x_scales[:, 4 * q : 4 * q + 4, :].bitcast(I32),
+            )
+        picks = keep.tile([P, S // 16], U16, name="picks")
+        nc.sync.dma_start(picks[:], offs)
+        word_tables = []
+        for g in range(PASSES):
+            table = keep.tile([P, T], U32, name="word_table%d" % g, align_bytes=64)
+            nc.sync.dma_start(table[:].bitcast(I32), x_words[g].rearrange("p c t -> p (c t)").bitcast(I32))
+            word_tables.append(table)
+        nc.sync.dma_start(cond_rows[0:BLOCKS], cond[:, 0, :].rearrange("d (b j) -> b d j", b=BLOCKS))
+        lists, conds = [], []
+        for d, pos in enumerate((pos1, pos2, pos3)):
+            neighbours = keep.tile([P, S // 16], U16, name="neighbours%d" % d)
+            nc.sync.dma_start(neighbours[:], pos)
+            lists.append(neighbours)
+            c = keep.tile([P, S], F32, name="cond%d" % d)
+            nc.sync.dma_start(c[:], cond[d])
+            conds.append(c)
+
+        w_bf = keep.tile([P, PASSES, N, PACK], BF16, name="w_bf", align_bytes=64)
+        for g in range(PASSES):
+            nc.scalar.activation(
+                w_bf[:, g].rearrange("p (c i) t -> p c t i", i=4),
+                w_raw[:, g].rearrange("p t (c i) -> p c t i", i=4),
+                ACT.Copy,
+            )
+        w_codes = keep.tile([P, PASSES * N], U32, name="w_codes", align_bytes=64)
+        w_scales = keep.tile([P, PASSES * N], U8, name="w_scales", align_bytes=64)
+
+        x_bytes = keep.tile([P, S], U8, name="x_bytes", align_bytes=64)
+        nc.vector.tensor_copy(x_bytes[:], scale_table[:].indirect(picks[:]))
+        nc.vector.quantize_mx(out=w_codes[:].bitcast(FP8X4), scales=w_scales[:], in_=w_bf[:].rearrange("p g n t -> p (g n t)"))
+        x_codes0 = keep.tile([P, S], U32, name="x_codes0", align_bytes=64)
+        nc.vector.tensor_copy(x_codes0[:], word_tables[0][:].indirect(picks[:]))
+
+        cond_sum = psum.tile([P, P], F32, name="cond_sum", tag="sum1")
+        for d in range(D):
+            nc.tensor.matmul(cond_sum[:], lhsT=cond_rows[:, d, :], rhs=ident[:], is_transpose=True, start=(d == 0), stop=(d == D - 1))
+        outflow = keep.tile([P, BLOCKS], F32, name="outflow")
+        nc.scalar.activation(outflow[:], cond_sum[:, 0:BLOCKS], ACT.Copy, scale=-1.0)
+
+        ent0 = keep.tile([P, S], F32, name="ent0")
+        tm0 = keep.tile([P, S], F32, name="tm0")
+        above0 = keep.tile([P, S], F32, name="above0")
+        for h in range(2):
+            x_codes1 = keep.tile([P, HALF], U32, name="x_codes1_%d" % h, align_bytes=64)
+            nc.vector.tensor_copy(x_codes1[:], word_tables[1][:].indirect(picks[:, entries(h)]))
+            y = psum.tile([P, HALF], F32, name="y%d" % h)
+            for g, codes in enumerate((x_codes0[:, cols(h)], x_codes1[:])):
+                nc.tensor.matmul_mx(
+                    out=y[:],
+                    lhsT=w_codes[:, block(g)].bitcast(FP8X4),
+                    lhsT_scale=w_scales[:, block(g)],
+                    rhs=codes.bitcast(FP8X4),
+                    rhs_scale=x_bytes[4 * g : P, cols(h)],
+                    start=(g == 0),
+                    stop=(g == PASSES - 1),
+                )
+            nc.scalar.activation(above0[:, cols(h)], y[:], ACT.Relu, bias=-LATENT)
+            nc.vector.tensor_tensor(tm0[:, cols(h)], y[:], above0[:, cols(h)], ALU.min)
+            nc.scalar.copy(ent0[:, cols(h)], y[:])
+
+        def step(name, ent, tm):
+            lost = keep.tile([P, S], F32, name=name + "lost")
+            turned = keep.tile([P, S], F32, name=name + "turned")
+            flows = [keep.tile([P, S], F32, name=name + "flow%d" % d) for d in range(D)]
+            partial, total = [], []
+            for h in range(2):
+                tm_t = psum.tile([P, HALF], F32, name=name + "tm_t%d" % h, tag="tm_t%d" % h)
+                for b in range(2):
+                    nc.tensor.transpose(tm_t[:, block(b)], tm[:, block(2 * h + b)], ident[:])
+                for b in range(2):
+                    nc.scalar.activation(lost[:, block(2 * h + b)], tm_t[:, block(b)], ACT.Copy, scale=outflow[:, 2 * h + b : 2 * h + b + 1])
+            for h in range(2):
+                acc = psum.tile([P, HALF], F32, name=name + "acc%d" % h, tag="acc%d" % h)
+                for b in range(2):
+                    nc.tensor.matmul(acc[:, block(b)], lhsT=ent[:, block(2 * h + b)], rhs=ident[:], is_transpose=True, start=(b == 0), stop=False)
+                partial.append(acc)
+            for h in range(2):
+                back = psum.tile([P, HALF], F32, name=name + "sum%d" % h, tag="sum%d" % h)
+                for b in range(2):
+                    nc.tensor.matmul(back[:, block(b)], lhsT=lost[:, block(2 * h + b)], rhs=ident[:], is_transpose=True, start=(b == 0), stop=False)
+                total.append(back)
+            for d in range(D):
+                for h in range(2):
+                    nc.vector.tensor_tensor(flows[d][:, cols(h)], tm[:].indirect(lists[d][:, entries(h)]), conds[d][:, cols(h)], ALU.mult)
+                    if d < D - 1:
+                        for b in range(2):
+                            nc.tensor.matmul(partial[h][:, block(b)], lhsT=flows[d][:, block(2 * h + b)], rhs=ident[:], is_transpose=True, start=False, stop=(d == D - 2 and b == 1))
+                    if d == D - 2:
+                        nc.scalar.copy(turned[:, cols(h)], partial[h][:])
+                        for b in range(2):
+                            nc.tensor.matmul(total[h][:, block(b)], lhsT=turned[:, block(2 * h + b)], rhs=ident[:], is_transpose=True, start=False, stop=(b == 1))
+            return total, flows[D - 1]
+
+        total, last = step("a", ent0, tm0)
+        ent1 = keep.tile([P, S], F32, name="ent1")
+        tm1 = keep.tile([P, S], F32, name="tm1")
+        part1 = keep.tile([P, S], F32, name="part1")
+        nc.vector.tensor_tensor(ent1[:, cols(0)], total[0][:], last[:, cols(0)], ALU.add)
+        nc.scalar.activation(part1[:, cols(0)], ent1[:, cols(0)], ACT.Relu, bias=-LATENT)
+        nc.vector.tensor_tensor(ent1[:, cols(1)], total[1][:], last[:, cols(1)], ALU.add)
+        nc.vector.tensor_tensor(tm1[:, cols(0)], ent1[:, cols(0)], part1[:, cols(0)], ALU.min)
+        nc.vector.tensor_scalar(part1[:, cols(1)], ent1[:, cols(1)], 0.0, None, ALU.min)
+        nc.vector.scalar_tensor_tensor(tm1[:, cols(1)], ent1[:, cols(1)], LATENT, part1[:, cols(1)], ALU.subtract, ALU.max)
+
+        total, last = step("b", ent1, tm1)
+        for h in range(2):
+            result = keep.tile([P, HALF], F32, name="result%d" % h)
+            nc.vector.tensor_tensor(result[:], total[h][:], last[:, cols(h)], ALU.add)
+            nc.sync.dma_start(out[:, cols(h)], result[:])

@@ -22,6 +22,7 @@ PASSES = K // (P * PACK)
 HALF = S // 2
 BLOCKS = S // P
 LATENT = 0.6
+PIECES = (slice(0, HALF), slice(HALF, HALF + P), slice(HALF + P, S))
 
 
 def tile_picked_ystefn_two_p_kernel(tc, x_words, x_scales, w1, cond, offs, pos1, pos2, pos3, out):
@@ -48,18 +49,24 @@ def tile_picked_ystefn_two_p_kernel(tc, x_words, x_scales, w1, cond, offs, pos1,
 
         w_raw = keep.tile([P, PASSES, PACK, N], F32, name="w_raw")
         nc.sync.dma_start(w_raw[:], w1.rearrange("(g p t) n -> p g t n", g=PASSES, t=PACK))
-        for q in range(4):
-            nc.sync.dma_start(
-                scale_table[32 * q : 32 * q + 4 * PASSES, :].bitcast(I32),
-                x_scales[:, 4 * q : 4 * q + 4, :].bitcast(I32),
-            )
-        picks = keep.tile([P, S // 16], U16, name="picks")
-        nc.sync.dma_start(picks[:], offs)
-        word_tables = []
-        for g in range(PASSES):
+
+        def load_scale_rows(i):
+            r, g = divmod(i, PASSES)
+            nc.sync.dma_start(scale_table[4 * g + r : P : 32, :].bitcast(I32), x_scales[g, r:16:4, :].bitcast(I32))
+
+        def load_words(g):
             table = keep.tile([P, T], U32, name="word_table%d" % g, align_bytes=64)
             nc.sync.dma_start(table[:].bitcast(I32), x_words[g].rearrange("p c t -> p (c t)").bitcast(I32))
-            word_tables.append(table)
+            return table
+
+        picks = keep.tile([P, S // 16], U16, name="picks")
+        nc.sync.dma_start(picks[:], offs)
+        for i in range(5):
+            load_scale_rows(i)
+        word_tables = [load_words(0)]
+        for i in range(5, 8):
+            load_scale_rows(i)
+        word_tables.append(load_words(1))
         nc.sync.dma_start(cond_rows[0:BLOCKS], cond[:, 0, :].rearrange("d (b j) -> b d j", b=BLOCKS))
         lists, conds = [], []
         for d, pos in enumerate((pos1, pos2, pos3)):
@@ -80,85 +87,112 @@ def tile_picked_ystefn_two_p_kernel(tc, x_words, x_scales, w1, cond, offs, pos1,
         w_codes = keep.tile([P, PASSES * N], U32, name="w_codes", align_bytes=64)
         w_scales = keep.tile([P, PASSES * N], U8, name="w_scales", align_bytes=64)
 
-        x_bytes = keep.tile([P, S], U8, name="x_bytes", align_bytes=64)
-        nc.vector.tensor_copy(x_bytes[:], scale_table[:].indirect(picks[:]))
         nc.vector.quantize_mx(out=w_codes[:].bitcast(FP8X4), scales=w_scales[:], in_=w_bf[:].rearrange("p g n t -> p (g n t)"))
         x_codes0 = keep.tile([P, S], U32, name="x_codes0", align_bytes=64)
         nc.vector.tensor_copy(x_codes0[:], word_tables[0][:].indirect(picks[:]))
+        x_bytes = keep.tile([P, S], U8, name="x_bytes", align_bytes=64)
+        nc.vector.tensor_copy(x_bytes[:], scale_table[:].indirect(picks[:]))
 
-        cond_sum = psum.tile([P, P], F32, name="cond_sum", tag="sum1")
+        def turn(dst, src, start, stop):
+            nc.tensor.matmul(dst, lhsT=src, rhs=ident[:], is_transpose=True, start=start, stop=stop)
+
+        def product(y, g, piece, codes):
+            nc.tensor.matmul_mx(
+                out=y[:],
+                lhsT=w_codes[:, block(g)].bitcast(FP8X4),
+                lhsT_scale=w_scales[:, block(g)],
+                rhs=codes[:, piece].bitcast(FP8X4),
+                rhs_scale=x_bytes[4 * g : P, piece],
+                start=(g == 0),
+                stop=(g == PASSES - 1),
+            )
+
+        def blocks(piece):
+            return range(piece.start // P, piece.stop // P)
+
+        def temperature_tile(name):
+            tm = keep.tile([P, S], F32, name=name)
+            return tm
+
+        ys = [psum.tile([P, piece.stop - piece.start], F32, name="y%d" % i, tag="total%d" % i) for i, piece in enumerate(PIECES)]
+        for y, piece in zip(ys, PIECES):
+            product(y, 0, piece, x_codes0)
+
+        cond_sum = psum.tile([P, P], F32, name="cond_sum", tag="tm_t1")
         for d in range(D):
-            nc.tensor.matmul(cond_sum[:], lhsT=cond_rows[:, d, :], rhs=ident[:], is_transpose=True, start=(d == 0), stop=(d == D - 1))
+            turn(cond_sum[:], cond_rows[:, d, :], d == 0, d == D - 1)
         outflow = keep.tile([P, BLOCKS], F32, name="outflow")
         nc.scalar.activation(outflow[:], cond_sum[:, 0:BLOCKS], ACT.Copy, scale=-1.0)
 
-        ent0 = keep.tile([P, S], F32, name="ent0")
-        tm0 = keep.tile([P, S], F32, name="tm0")
-        above0 = keep.tile([P, S], F32, name="above0")
+        x_codes1 = keep.tile([P, S], U32, name="x_codes1", align_bytes=64)
         for h in range(2):
-            x_codes1 = keep.tile([P, HALF], U32, name="x_codes1_%d" % h, align_bytes=64)
-            nc.vector.tensor_copy(x_codes1[:], word_tables[1][:].indirect(picks[:, entries(h)]))
-            y = psum.tile([P, HALF], F32, name="y%d" % h)
-            for g, codes in enumerate((x_codes0[:, cols(h)], x_codes1[:])):
-                nc.tensor.matmul_mx(
-                    out=y[:],
-                    lhsT=w_codes[:, block(g)].bitcast(FP8X4),
-                    lhsT_scale=w_scales[:, block(g)],
-                    rhs=codes.bitcast(FP8X4),
-                    rhs_scale=x_bytes[4 * g : P, cols(h)],
-                    start=(g == 0),
-                    stop=(g == PASSES - 1),
-                )
-            nc.scalar.activation(above0[:, cols(h)], y[:], ACT.Relu, bias=-LATENT)
-            nc.vector.tensor_tensor(tm0[:, cols(h)], y[:], above0[:, cols(h)], ALU.min)
-            nc.scalar.copy(ent0[:, cols(h)], y[:])
+            nc.vector.tensor_copy(x_codes1[:, cols(h)], word_tables[1][:].indirect(picks[:, entries(h)]))
+        ent0 = keep.tile([P, S], F32, name="ent0")
+        tm0 = temperature_tile("tm0")
+        above0 = keep.tile([P, S], F32, name="above0")
+        for y, piece in zip(ys, PIECES):
+            product(y, 1, piece, x_codes1)
+        for y, piece in zip(ys, PIECES):
+            nc.scalar.activation(above0[:, piece], y[:], ACT.Relu, bias=-LATENT)
+        for y, piece in zip(ys, PIECES):
+            nc.vector.tensor_tensor(tm0[:, piece], y[:], above0[:, piece], ALU.min)
+        for y, piece in zip(ys, PIECES):
+            nc.scalar.copy(ent0[:, piece], y[:])
 
         def step(name, ent, tm):
+            def gather(d, span):
+                offsets = lists[d][:, span.start // 16 : span.stop // 16]
+                nc.vector.tensor_tensor(flows[d][:, span], tm[:].indirect(offsets), conds[d][:, span], ALU.mult)
+
             lost = keep.tile([P, S], F32, name=name + "lost")
             turned = keep.tile([P, S], F32, name=name + "turned")
             flows = [keep.tile([P, S], F32, name=name + "flow%d" % d) for d in range(D)]
-            partial, total = [], []
+            accs, totals = [], []
+            for i, piece in enumerate(PIECES):
+                acc = psum.tile([P, S], F32, name=name + "acc%d" % i, tag="acc%d" % i)
+                for b in blocks(piece):
+                    turn(acc[:, block(b)], ent[:, block(b)], b == blocks(piece)[0], False)
+                accs.append(acc)
             for h in range(2):
-                tm_t = psum.tile([P, HALF], F32, name=name + "tm_t%d" % h, tag="tm_t%d" % h)
-                for b in range(2):
-                    nc.tensor.transpose(tm_t[:, block(b)], tm[:, block(2 * h + b)], ident[:])
-                for b in range(2):
-                    nc.scalar.activation(lost[:, block(2 * h + b)], tm_t[:, block(b)], ACT.Copy, scale=outflow[:, 2 * h + b : 2 * h + b + 1])
+                tm_t = psum.tile([P, S], F32, name=name + "tm_t%d" % h, tag="tm_t%d" % h)
+                for b in blocks(cols(h)):
+                    turn(tm_t[:, block(b)], tm[:, block(b)], True, True)
+                for b in blocks(cols(h)):
+                    nc.scalar.activation(lost[:, block(b)], tm_t[:, block(b)], ACT.Copy, scale=outflow[:, b : b + 1])
+            for i, piece in enumerate(PIECES):
+                total = psum.tile([P, S], F32, name=name + "total%d" % i, tag="total%d" % i)
+                for b in blocks(piece):
+                    turn(total[:, block(b)], lost[:, block(b)], b == blocks(piece)[0], False)
+                totals.append(total)
+            for acc, piece in zip(accs, PIECES):
+                if piece.start % HALF == 0:
+                    half = cols(piece.start // HALF)
+                    gather(0, half)
+                for b in blocks(piece):
+                    turn(acc[:, block(b)], flows[0][:, block(b)], False, False)
+                gather(1, piece)
+                for b in blocks(piece):
+                    turn(acc[:, block(b)], flows[1][:, block(b)], False, b == blocks(piece)[-1])
+                nc.scalar.copy(turned[:, piece], acc[:, piece])
+            for total, piece in zip(totals, PIECES):
+                for b in blocks(piece):
+                    turn(total[:, block(b)], turned[:, block(b)], False, b == blocks(piece)[-1])
             for h in range(2):
-                acc = psum.tile([P, HALF], F32, name=name + "acc%d" % h, tag="acc%d" % h)
-                for b in range(2):
-                    nc.tensor.matmul(acc[:, block(b)], lhsT=ent[:, block(2 * h + b)], rhs=ident[:], is_transpose=True, start=(b == 0), stop=False)
-                partial.append(acc)
-            for h in range(2):
-                back = psum.tile([P, HALF], F32, name=name + "sum%d" % h, tag="sum%d" % h)
-                for b in range(2):
-                    nc.tensor.matmul(back[:, block(b)], lhsT=lost[:, block(2 * h + b)], rhs=ident[:], is_transpose=True, start=(b == 0), stop=False)
-                total.append(back)
-            for d in range(D):
-                for h in range(2):
-                    nc.vector.tensor_tensor(flows[d][:, cols(h)], tm[:].indirect(lists[d][:, entries(h)]), conds[d][:, cols(h)], ALU.mult)
-                    if d < D - 1:
-                        for b in range(2):
-                            nc.tensor.matmul(partial[h][:, block(b)], lhsT=flows[d][:, block(2 * h + b)], rhs=ident[:], is_transpose=True, start=False, stop=(d == D - 2 and b == 1))
-                    if d == D - 2:
-                        nc.scalar.copy(turned[:, cols(h)], partial[h][:])
-                        for b in range(2):
-                            nc.tensor.matmul(total[h][:, block(b)], lhsT=turned[:, block(2 * h + b)], rhs=ident[:], is_transpose=True, start=False, stop=(b == 1))
-            return total, flows[D - 1]
+                gather(2, cols(h))
+            return totals, flows[2]
 
-        total, last = step("a", ent0, tm0)
         ent1 = keep.tile([P, S], F32, name="ent1")
-        tm1 = keep.tile([P, S], F32, name="tm1")
-        part1 = keep.tile([P, S], F32, name="part1")
-        nc.vector.tensor_tensor(ent1[:, cols(0)], total[0][:], last[:, cols(0)], ALU.add)
-        nc.scalar.activation(part1[:, cols(0)], ent1[:, cols(0)], ACT.Relu, bias=-LATENT)
-        nc.vector.tensor_tensor(ent1[:, cols(1)], total[1][:], last[:, cols(1)], ALU.add)
-        nc.vector.tensor_tensor(tm1[:, cols(0)], ent1[:, cols(0)], part1[:, cols(0)], ALU.min)
-        nc.vector.tensor_scalar(part1[:, cols(1)], ent1[:, cols(1)], 0.0, None, ALU.min)
-        nc.vector.scalar_tensor_tensor(tm1[:, cols(1)], ent1[:, cols(1)], LATENT, part1[:, cols(1)], ALU.subtract, ALU.max)
-
-        total, last = step("b", ent1, tm1)
-        for h in range(2):
-            result = keep.tile([P, HALF], F32, name="result%d" % h)
-            nc.vector.tensor_tensor(result[:], total[h][:], last[:, cols(h)], ALU.add)
-            nc.sync.dma_start(out[:, cols(h)], result[:])
+        tm1 = temperature_tile("tm1")
+        above1 = keep.tile([P, S], F32, name="above1")
+        totals, last = step("a", ent0, tm0)
+        for total, piece in zip(totals, PIECES):
+            nc.vector.tensor_tensor(ent1[:, piece], total[:, piece], last[:, piece], ALU.add)
+        nc.scalar.activation(above1[:, cols(0)], ent1[:, cols(0)], ACT.Relu, bias=-LATENT)
+        nc.vector.tensor_scalar(above1[:, cols(1)], ent1[:, cols(1)], 0.0, None, ALU.min)
+        nc.vector.scalar_tensor_tensor(tm1[:, cols(1)], ent1[:, cols(1)], LATENT, above1[:, cols(1)], ALU.subtract, ALU.max)
+        nc.vector.tensor_tensor(tm1[:, cols(0)], ent1[:, cols(0)], above1[:, cols(0)], ALU.min)
+        totals, last = step("b", ent1, tm1)
+        result = keep.tile([P, S], F32, name="result")
+        for total, piece in zip(totals, PIECES):
+            nc.vector.tensor_tensor(result[:, piece], total[:, piece], last[:, piece], ALU.add)
+            nc.sync.dma_start(out[:, piece], result[:, piece])

from contextlib import ExitStack

import concourse.mybir as mybir
from concourse.masks import make_identity

K, T, S, N, D = 1024, 2048, 512, 128, 3
FLOPS = 2 * K * S * N

F32 = mybir.dt.float32
BF16 = mybir.dt.bfloat16
I32 = mybir.dt.int32
U32 = mybir.dt.uint32
U16 = mybir.dt.uint16
U8 = mybir.dt.uint8
FP8X4 = mybir.dt.float8_e4m3fn_x4
ALU = mybir.AluOpType
ACT = mybir.ActivationFunctionType

P = 128
PACK = 4
PASSES = K // (P * PACK)
HALF = S // 2
BLOCKS = S // P
LATENT = 0.6
PIECES = (slice(0, HALF), slice(HALF, HALF + P), slice(HALF + P, S))


def tile_picked_ystefn_two_p_kernel(tc, x_words, x_scales, w1, cond, offs, pos1, pos2, pos3, out):
    nc = tc.nc
    with ExitStack() as ctx:
        keep = ctx.enter_context(tc.tile_pool(name="keep", bufs=1))
        psum = ctx.enter_context(tc.psum_pool(name="psum", bufs=1))

        def cols(h):
            return slice(h * HALF, (h + 1) * HALF)

        def entries(h):
            return slice(h * HALF // 16, (h + 1) * HALF // 16)

        def block(b):
            return slice(b * P, (b + 1) * P)

        scale_table = keep.tile([P, T], U8, name="scale_table", align_bytes=64)
        nc.vector.memset(scale_table[:].bitcast(I32), 0)
        cond_rows = keep.tile([P, D, P], F32, name="cond_rows")
        nc.vector.memset(cond_rows[:], 0.0)
        ident = keep.tile([P, P], F32, name="ident")
        make_identity(nc, ident[:])

        w_raw = keep.tile([P, PASSES, PACK, N], F32, name="w_raw")
        nc.sync.dma_start(w_raw[:], w1.rearrange("(g p t) n -> p g t n", g=PASSES, t=PACK))

        def load_scale_rows(i):
            r, g = divmod(i, PASSES)
            nc.sync.dma_start(scale_table[4 * g + r : P : 32, :].bitcast(I32), x_scales[g, r:16:4, :].bitcast(I32))

        def load_words(g):
            table = keep.tile([P, T], U32, name="word_table%d" % g, align_bytes=64)
            nc.sync.dma_start(table[:].bitcast(I32), x_words[g].rearrange("p c t -> p (c t)").bitcast(I32))
            return table

        picks = keep.tile([P, S // 16], U16, name="picks")
        nc.sync.dma_start(picks[:], offs)
        for i in range(5):
            load_scale_rows(i)
        word_tables = [load_words(0)]
        for i in range(5, 8):
            load_scale_rows(i)
        word_tables.append(load_words(1))
        nc.sync.dma_start(cond_rows[0:BLOCKS], cond[:, 0, :].rearrange("d (b j) -> b d j", b=BLOCKS))
        lists, conds = [], []
        for d, pos in enumerate((pos1, pos2, pos3)):
            neighbours = keep.tile([P, S // 16], U16, name="neighbours%d" % d)
            nc.sync.dma_start(neighbours[:], pos)
            lists.append(neighbours)
            c = keep.tile([P, S], F32, name="cond%d" % d)
            nc.sync.dma_start(c[:], cond[d])
            conds.append(c)

        w_bf = keep.tile([P, PASSES, N, PACK], BF16, name="w_bf", align_bytes=64)
        for g in range(PASSES):
            nc.scalar.activation(
                w_bf[:, g].rearrange("p (c i) t -> p c t i", i=4),
                w_raw[:, g].rearrange("p t (c i) -> p c t i", i=4),
                ACT.Copy,
            )
        w_codes = keep.tile([P, PASSES * N], U32, name="w_codes", align_bytes=64)
        w_scales = keep.tile([P, PASSES * N], U8, name="w_scales", align_bytes=64)

        nc.vector.quantize_mx(out=w_codes[:].bitcast(FP8X4), scales=w_scales[:], in_=w_bf[:].rearrange("p g n t -> p (g n t)"))
        x_codes0 = keep.tile([P, S], U32, name="x_codes0", align_bytes=64)
        nc.vector.tensor_copy(x_codes0[:], word_tables[0][:].indirect(picks[:]))
        x_bytes = keep.tile([P, S], U8, name="x_bytes", align_bytes=64)
        nc.vector.tensor_copy(x_bytes[:], scale_table[:].indirect(picks[:]))

        def turn(dst, src, start, stop):
            nc.tensor.matmul(dst, lhsT=src, rhs=ident[:], is_transpose=True, start=start, stop=stop)

        def product(y, g, piece, codes):
            nc.tensor.matmul_mx(
                out=y[:],
                lhsT=w_codes[:, block(g)].bitcast(FP8X4),
                lhsT_scale=w_scales[:, block(g)],
                rhs=codes[:, piece].bitcast(FP8X4),
                rhs_scale=x_bytes[4 * g : P, piece],
                start=(g == 0),
                stop=(g == PASSES - 1),
            )

        def blocks(piece):
            return range(piece.start // P, piece.stop // P)

        def temperature_tile(name):
            tm = keep.tile([P, S], F32, name=name)
            return tm

        ys = [psum.tile([P, piece.stop - piece.start], F32, name="y%d" % i, tag="total%d" % i) for i, piece in enumerate(PIECES)]
        for y, piece in zip(ys, PIECES):
            product(y, 0, piece, x_codes0)

        cond_sum = psum.tile([P, P], F32, name="cond_sum", tag="tm_t1")
        for d in range(D):
            turn(cond_sum[:], cond_rows[:, d, :], d == 0, d == D - 1)
        outflow = keep.tile([P, BLOCKS], F32, name="outflow")
        nc.scalar.activation(outflow[:], cond_sum[:, 0:BLOCKS], ACT.Copy, scale=-1.0)

        x_codes1 = keep.tile([P, S], U32, name="x_codes1", align_bytes=64)
        for h in range(2):
            nc.vector.tensor_copy(x_codes1[:, cols(h)], word_tables[1][:].indirect(picks[:, entries(h)]))
        ent0 = keep.tile([P, S], F32, name="ent0")
        tm0 = temperature_tile("tm0")
        above0 = keep.tile([P, S], F32, name="above0")
        for y, piece in zip(ys, PIECES):
            product(y, 1, piece, x_codes1)
        for y, piece in zip(ys, PIECES):
            nc.scalar.activation(above0[:, piece], y[:], ACT.Relu, bias=-LATENT)
        for y, piece in zip(ys, PIECES):
            nc.vector.tensor_tensor(tm0[:, piece], y[:], above0[:, piece], ALU.min)
        for y, piece in zip(ys, PIECES):
            nc.scalar.copy(ent0[:, piece], y[:])

        def step(name, ent, tm):
            def gather(d, span):
                offsets = lists[d][:, span.start // 16 : span.stop // 16]
                nc.vector.tensor_tensor(flows[d][:, span], tm[:].indirect(offsets), conds[d][:, span], ALU.mult)

            lost = keep.tile([P, S], F32, name=name + "lost")
            turned = keep.tile([P, S], F32, name=name + "turned")
            flows = [keep.tile([P, S], F32, name=name + "flow%d" % d) for d in range(D)]
            accs, totals = [], []
            for i, piece in enumerate(PIECES):
                acc = psum.tile([P, S], F32, name=name + "acc%d" % i, tag="acc%d" % i)
                for b in blocks(piece):
                    turn(acc[:, block(b)], ent[:, block(b)], b == blocks(piece)[0], False)
                accs.append(acc)
            for h in range(2):
                tm_t = psum.tile([P, S], F32, name=name + "tm_t%d" % h, tag="tm_t%d" % h)
                for b in blocks(cols(h)):
                    turn(tm_t[:, block(b)], tm[:, block(b)], True, True)
                for b in blocks(cols(h)):
                    nc.scalar.activation(lost[:, block(b)], tm_t[:, block(b)], ACT.Copy, scale=outflow[:, b : b + 1])
            for i, piece in enumerate(PIECES):
                total = psum.tile([P, S], F32, name=name + "total%d" % i, tag="total%d" % i)
                for b in blocks(piece):
                    turn(total[:, block(b)], lost[:, block(b)], b == blocks(piece)[0], False)
                totals.append(total)
            for acc, piece in zip(accs, PIECES):
                if piece.start % HALF == 0:
                    half = cols(piece.start // HALF)
                    gather(0, half)
                for b in blocks(piece):
                    turn(acc[:, block(b)], flows[0][:, block(b)], False, False)
                gather(1, piece)
                for b in blocks(piece):
                    turn(acc[:, block(b)], flows[1][:, block(b)], False, b == blocks(piece)[-1])
                nc.scalar.copy(turned[:, piece], acc[:, piece])
            for total, piece in zip(totals, PIECES):
                for b in blocks(piece):
                    turn(total[:, block(b)], turned[:, block(b)], False, b == blocks(piece)[-1])
            for h in range(2):
                gather(2, cols(h))
            return totals, flows[2]

        ent1 = keep.tile([P, S], F32, name="ent1")
        tm1 = temperature_tile("tm1")
        above1 = keep.tile([P, S], F32, name="above1")
        totals, last = step("a", ent0, tm0)
        for total, piece in zip(totals, PIECES):
            nc.vector.tensor_tensor(ent1[:, piece], total[:, piece], last[:, piece], ALU.add)
        nc.scalar.activation(above1[:, cols(0)], ent1[:, cols(0)], ACT.Relu, bias=-LATENT)
        nc.vector.tensor_scalar(above1[:, cols(1)], ent1[:, cols(1)], 0.0, None, ALU.min)
        nc.vector.scalar_tensor_tensor(tm1[:, cols(1)], ent1[:, cols(1)], LATENT, above1[:, cols(1)], ALU.subtract, ALU.max)
        nc.vector.tensor_tensor(tm1[:, cols(0)], ent1[:, cols(0)], above1[:, cols(0)], ALU.min)
        totals, last = step("b", ent1, tm1)
        result = keep.tile([P, S], F32, name="result")
        for total, piece in zip(totals, PIECES):
            nc.vector.tensor_tensor(result[:, piece], total[:, piece], last[:, piece], ALU.add)
            nc.sync.dma_start(out[:, piece], result[:, piece])
